import numpy as np
import ml_dtypes


def mxq(x, axis, fmt="e4m3"):
    dtype, down = {"e4m3": (ml_dtypes.float8_e4m3fn, 7), "e5m2": (ml_dtypes.float8_e5m2, 14)}[fmt]
    v = np.moveaxis(np.asarray(x, np.float32).astype(ml_dtypes.bfloat16).astype(np.float64), axis, -1)
    blocks = v.reshape(v.shape[:-1] + (-1, 32))
    amax = np.abs(blocks).max(-1, keepdims=True)
    byte = np.maximum(np.where(amax > 0, np.frexp(amax)[1] - 1 + 127, 0) - down, 1)
    scale = np.exp2(byte - 127.0)
    codes = (blocks / scale).astype(np.float32).astype(dtype).astype(np.float64)
    return np.moveaxis((codes * scale).reshape(v.shape), -1, axis)


WIDE = False


def mx_kscale(k):
    if not WIDE:
        return np.ones(k)
    levels = np.array([10, -10, 5, -5, 0])
    if k % 512:
        return np.exp2(np.random.permutation(np.resize(levels, k // 32))).repeat(32)
    a = np.empty((k // 512, 16))
    for p in range(k // 512):
        a[p, :8] = np.random.permutation(np.resize(levels, 8))
        for g in range(8):
            far = levels[np.abs(levels - a[p, g]) >= 10]
            a[p, g + 8] = far[np.random.randint(len(far))]
    return np.exp2(a.ravel()).repeat(32)


def f64(x):
    return np.asarray(x).astype(np.float64)


def striped8(idx):
    return np.asarray(idx).reshape(8, -1, 16).transpose(0, 2, 1).reshape(128, -1).astype(np.uint16)


def unstriped8(offs):
    return offs.reshape(8, 16, -1).transpose(0, 2, 1).reshape(8, -1).astype(np.int64)


def pick8(x, idx, run):
    r = np.arange(len(x))
    return x[r[:, None], idx[r % (8 * run) // run]]


E2M1 = np.array([0.0, 0.5, 1.0, 1.5, 2.0, 3.0, 4.0, 6.0, -0.0, -0.5, -1.0, -1.5, -2.0, -3.0, -4.0, -6.0])


def pack_weight(w, fmt):
    k, n = w.shape
    w = f64(np.asarray(w, np.float32).astype(ml_dtypes.bfloat16)).reshape(k // 32, 32, n)
    amax = np.abs(w).max(1)
    if fmt == "e4m3":
        byte = np.frexp(amax)[1] - 1 + 127 - 7
    else:
        mant, ex = np.frexp(amax / 6.0)
        byte = np.where(mant > 0.5, ex, ex - 1) + 127
    byte = np.clip(np.where(amax > 0, byte, 1), 1, 254)
    scaled = (w * np.exp2(127.0 - byte)[:, None, :]).reshape(k, n).astype(np.float32)
    by_word = np.ascontiguousarray(scaled.reshape(k // 512, 128, 4, n).transpose(0, 1, 3, 2))
    if fmt == "e4m3":
        words = by_word.astype(ml_dtypes.float8_e4m3fn).view(np.uint8)
    else:
        c = by_word.astype(ml_dtypes.float4_e2m1fn).view(np.uint8) & 0xF
        words = (c[..., 0::2] | (c[..., 1::2] << 4)).reshape(k // 512, 128, 2 * n)
    return np.ascontiguousarray(words), np.ascontiguousarray(byte.astype(np.uint8).reshape(k // 512, 16, n))


def unpack_weight(words, scales, fmt):
    g, _, n = scales.shape
    words = np.ascontiguousarray(words).reshape(g, 128, n, -1)
    if fmt == "e4m3":
        vals = words.view(ml_dtypes.float8_e4m3fn).astype(np.float64)
    else:
        nib = np.empty((g, 128, n, 4), np.uint8)
        nib[..., 0::2] = words & 0xF
        nib[..., 1::2] = words >> 4
        vals = E2M1[nib]
    vals = vals * np.repeat(np.exp2(scales.astype(np.float64) - 127.0), 8, axis=1)[..., None]
    return vals.transpose(0, 1, 3, 2).reshape(g * 512, n)


C, D, I, Z, J, Q = 512, 512, 256, 512, 256, 128


def setup_inputs():
    n = np.random.standard_normal
    idx = np.stack([np.random.permutation(Z)[:I] for _ in range(8)])
    idx2 = np.stack([np.random.permutation(Z)[:J] for _ in range(8)])
    idx3 = np.stack([np.random.permutation(Z)[:J] for _ in range(8)])
    idx4 = np.stack([np.random.permutation(Z)[:J] for _ in range(8)])
    idx5 = np.stack([np.random.permutation(Z)[:J] for _ in range(8)])
    fc = mx_kscale(C)
    fd = mx_kscale(D)
    wpp = pack_weight(n((C, D)) * 1.0 / np.sqrt(C) * fc[:, None] / fd, "e4m3")
    oldsp = pack_weight(n((C, Z)) / fc[:, None], "e2m1")
    wkp = pack_weight(n((C, D)) * 1.0 / np.sqrt(C) * fc[:, None] / fd, "e2m1")
    newsp = pack_weight(n((C, I)) / fc[:, None], "e4m3")
    return {
        "wp_words": wpp[0],
        "wp_scales": wpp[1],
        "olds_words": oldsp[0],
        "olds_scales": oldsp[1],
        "wk_words": wkp[0],
        "wk_scales": wkp[1],
        "news_words": newsp[0],
        "news_scales": newsp[1],
        "query": (n((D, Q)) * 1.0 / np.sqrt(D) * fd[:, None]).astype(np.float32),
        "offs": striped8(idx),
        "offs2": striped8(idx2),
        "offs3": striped8(idx3),
        "offs4": striped8(idx4),
        "offs5": striped8(idx5),
    }


def reference(wp_words, wp_scales, olds_words, olds_scales, wk_words, wk_scales, news_words, news_scales, query, offs, offs2, offs3, offs4, offs5):
    idx = unstriped8(offs)
    idx2 = unstriped8(offs2)
    idx3 = unstriped8(offs3)
    idx4 = unstriped8(offs4)
    idx5 = unstriped8(offs5)
    wpu = unpack_weight(wp_words, wp_scales, "e4m3")
    oldsu = unpack_weight(olds_words, olds_scales, "e2m1")
    wku = unpack_weight(wk_words, wk_scales, "e2m1")
    newsu = unpack_weight(news_words, news_scales, "e4m3")
    kb = wpu.T @ oldsu
    kn = wku.T @ newsu
    f1 = np.zeros((D, Z))
    f1[np.arange(D)[:, None], idx[np.arange(D) % 512 // 64]] = kn
    w = np.maximum(pick8(f1, idx2, 64), pick8(kb, idx3, 64))
    f2 = np.zeros((D, Z))
    f2[np.arange(D)[:, None], idx3[np.arange(D) % 512 // 64]] = w
    pg = kb - f2
    queryq = mxq(f64(query), 0, "e4m3")
    pgq = mxq(pg, 0, "e4m3")
    s = queryq.T @ pgq
    y = pick8(s, idx4, 16) * 2.0 - pick8(s, idx5, 16)
    return y

@@ -1,0 +1,202 @@
+from contextlib import ExitStack
+
+import concourse.mybir as mybir
+
+F32 = mybir.dt.float32
+BF16 = mybir.dt.bfloat16
+I32 = mybir.dt.int32
+U32 = mybir.dt.uint32
+U16 = mybir.dt.uint16
+U8 = mybir.dt.uint8
+FP8X4 = mybir.dt.float8_e4m3fn_x4
+FP4X4 = mybir.dt.float4_e2m1fn_x4
+ALU = mybir.AluOpType
+COPY = mybir.ActivationFunctionType.Copy
+
+C, D, I, Z, J, Q = 512, 512, 256, 512, 256, 128
+P = 128
+PLACES = 4
+RUN = 4
+HALF = Z // 2
+
+FLOPS = 2 * C * D * Z + 2 * C * D * I + 2 * D * Q * Z
+
+
+def tile_attend_headcarry_plainq_kernel(
+    tc, wp_words, wp_scales, olds_words, olds_scales, wk_words, wk_scales, news_words, news_scales,
+    query, offs, offs2, offs3, offs4, offs5, out,
+):
+    nc = tc.nc
+    with ExitStack() as ctx:
+        lists = ctx.enter_context(tc.tile_pool(name="lists", bufs=1))
+        sb = ctx.enter_context(tc.tile_pool(name="sb", bufs=1))
+        ps = ctx.enter_context(tc.psum_pool(name="ps", bufs=1))
+
+        def load_list(src, name):
+            t = lists.tile([P, 16], U16, name=name)
+            nc.sync.dma_start(t[:], src)
+            return t
+
+        def load_scale_rows(src, width, name, tag):
+            t = sb.tile([P, 2, width], U8, name=name, tag=tag, align_bytes=64)
+            nc.vector.memset(t[0:64].bitcast(I32), 0)
+            rows = src[0].bitcast(I32).rearrange("(h a f) c -> a f h c", h=2, a=2)
+            for a in range(2):
+                nc.sync.dma_start(t[32 * a : 32 * a + 4].bitcast(I32), rows[a])
+            return t
+
+        def load_scale_stage(src, width, name, tag):
+            t = sb.tile([4, 4, width // 4], I32, name=name, tag=tag, align_bytes=64)
+            nc.scalar.dma_start(t[:], src[0].bitcast(I32).rearrange("(a f) c -> f a c", f=4))
+            return t
+
+        def zeroed_plane(width, name):
+            t = sb.tile([P, width], U8, name=name, align_bytes=64)
+            nc.vector.memset(t[:].bitcast(I32), 0)
+            return t
+
+        def raise_upper(t):
+            nc.vector.tensor_copy(t[64:128, 0, :].bitcast(I32), t[0:64, 1, :].bitcast(I32))
+
+        def deal_scales(t, name):
+            plane = sb.tile([P, D], U8, name=name, align_bytes=64)
+            nc.vector.tensor_copy(
+                plane[:].bitcast(I32).rearrange("p (t g) -> p t g", t=PLACES),
+                t[:, 0, :].bitcast(I32).rearrange("p (g t) -> p t g", t=PLACES),
+            )
+            return plane
+
+        wk_rows = load_scale_stage(wk_scales, D, "wk_rows", "slot0")
+        news_rows = load_scale_stage(news_scales, I, "news_rows", "news_rows")
+        wk_raw = sb.tile([P, D // 2], I32, name="wk_raw", tag="slot1", align_bytes=64)
+        nc.sync.dma_start(wk_raw[:], wk_words[0].bitcast(I32))
+        news_codes = sb.tile([P, I], I32, name="news_codes", tag="slot3", align_bytes=64)
+        nc.sync.dma_start(news_codes[:], news_words[0].rearrange("p n t -> p (n t)").bitcast(I32))
+        fresh_slots = load_list(offs, "fresh_slots")
+        wp_raw = sb.tile([P, D], I32, name="wp_raw", tag="fresh_key")
+        nc.sync.dma_start(wp_raw[:], wp_words[0].rearrange("p n t -> p (n t)").bitcast(I32))
+        olds_codes = sb.tile([P, Z // 2], I32, name="olds_codes", align_bytes=64)
+        nc.sync.dma_start(olds_codes[:], olds_words[0].bitcast(I32))
+        wp_rows = load_scale_rows(wp_scales, D, "wp_rows", "wp_rows")
+        olds_rows = load_scale_rows(olds_scales, Z, "olds_rows", "olds_rows")
+        old_picks = load_list(offs3, "old_picks")
+        fresh_picks = load_list(offs2, "fresh_picks")
+        q_raw = sb.tile([P, PLACES, Q], F32, name="q_raw")
+        q_rows = query.rearrange("(g t r) q -> r g t q", t=PLACES, r=RUN)
+        for r in range(RUN):
+            nc.sync.dma_start(q_raw[r:P:RUN, :, :], q_rows[r])
+        plus_picks = load_list(offs4, "plus_picks")
+        minus_picks = load_list(offs5, "minus_picks")
+
+        wk_plane = zeroed_plane(D, "wk_plane")
+        news_plane = zeroed_plane(I, "news_plane")
+        f1 = [sb.tile([P, Z], F32, name="f1_%d" % t) for t in range(PLACES)]
+        for t in range(PLACES):
+            nc.vector.memset(f1[t][:], 0.0)
+
+        wk_codes = sb.tile([P, D], U16, name="wk_codes", tag="slot2", align_bytes=64)
+        nc.scalar.copy(
+            wk_codes[:].rearrange("p (t g r) -> p t g r", t=PLACES, r=RUN),
+            wk_raw[:].bitcast(U16).rearrange("p (g t r) -> p t g r", t=PLACES, r=RUN),
+        )
+        for a in range(4):
+            rows = slice(32 * a, 32 * a + 4)
+            nc.vector.tensor_copy(
+                wk_plane[rows, :].bitcast(I32).rearrange("f (t g) -> f t g", t=PLACES),
+                wk_rows[:, a, :].rearrange("f (g t) -> f t g", t=PLACES),
+            )
+            nc.vector.tensor_copy(news_plane[rows, :].bitcast(I32), news_rows[:, a, :])
+
+        kn_banks = [
+            ps.tile([P, 1, I], F32, name="kn_bank0", tag="bank_a"),
+            ps.tile([P, 1, I], F32, name="kn_bank1", tag="bank_b"),
+            ps.tile([P, 2, I], F32, name="kn_bank2", tag="bank_c"),
+        ]
+        kn_slot = [kn_banks[0][:, 0, :], kn_banks[1][:, 0, :], kn_banks[2][:, 0, :], kn_banks[2][:, 1, :]]
+        for t in range(PLACES):
+            cols = slice(t * P, (t + 1) * P)
+            nc.tensor.matmul_mx(
+                out=kn_slot[t], lhsT=wk_codes[:, cols].bitcast(FP4X4), lhsT_scale=wk_plane[:, cols],
+                rhs=news_codes[:].bitcast(FP8X4), rhs_scale=news_plane[:], start=True, stop=True,
+            )
+        kn0 = sb.tile([P, 1, I], F32, name="kn0")
+        kn1 = sb.tile([P, 1, I], F32, name="kn1")
+        kn23 = sb.tile([P, 2, I], F32, name="kn23")
+        nc.scalar.copy(kn0[:], kn_banks[0][:])
+        nc.vector.tensor_copy(kn1[:], kn_banks[1][:])
+        nc.vector.tensor_copy(kn23[:], kn_banks[2][:])
+        kn = [kn0[:, 0, :], kn1[:, 0, :], kn23[:, 0, :], kn23[:, 1, :]]
+        for t in range(PLACES):
+            nc.scalar.activation(f1[t][:].indirect(fresh_slots[:]), kn[t], COPY)
+
+        f2 = [sb.tile([P, Z], F32, name="f2_%d" % t, tag="slot%d" % t, align_bytes=64) for t in range(PLACES)]
+        for t in range(PLACES):
+            nc.vector.memset(f2[t][:], 0.0)
+
+        raise_upper(wp_rows)
+        raise_upper(olds_rows)
+        wp_codes = sb.tile([P, D], I32, name="wp_codes", align_bytes=64)
+        nc.vector.tensor_copy(
+            wp_codes[:].rearrange("p (t g r) -> p t g r", t=PLACES, r=RUN),
+            wp_raw[:].rearrange("p (g t r) -> p t g r", t=PLACES, r=RUN),
+        )
+        wp_plane = deal_scales(wp_rows, "wp_plane")
+        kb_banks = [ps.tile([P, Z], F32, name="kb_bank%d" % t) for t in range(PLACES)]
+        for t in range(PLACES):
+            cols = slice(t * P, (t + 1) * P)
+            nc.tensor.matmul_mx(
+                out=kb_banks[t][:], lhsT=wp_codes[:, cols].bitcast(FP8X4), lhsT_scale=wp_plane[:, cols],
+                rhs=olds_codes[:].bitcast(U16).bitcast(FP4X4), rhs_scale=olds_rows[:, 0, :], start=True, stop=True,
+            )
+        kb = [sb.tile([P, Z], F32, name="kb%d" % t) for t in range(PLACES)]
+        old_key = [sb.tile([P, J], F32, name="old_key%d" % t, tag="old_key%d" % t) for t in range(PLACES)]
+        w = [sb.tile([P, J], F32, name="w%d" % t) for t in range(PLACES)]
+        nc.vector.tensor_copy(kb[0][:], kb_banks[0][:])
+        for t in range(PLACES):
+            nc.vector.tensor_copy(old_key[t][:], kb[t][:].indirect(old_picks[:]))
+            fresh_key = sb.tile([P, J], F32, name="fresh_key", tag="fresh_key")
+            nc.vector.tensor_copy(fresh_key[:], f1[t][:].indirect(fresh_picks[:]))
+            if t + 1 < PLACES:
+                nc.vector.tensor_copy(kb[t + 1][:], kb_banks[t + 1][:])
+            nc.vector.tensor_tensor(w[t][:], fresh_key[:], old_key[t][:], ALU.max)
+            nc.scalar.activation(f2[t][:].indirect(old_picks[:]), w[t][:], COPY)
+
+        q_in = sb.tile([P, Q, PLACES], BF16, name="q_in", align_bytes=64)
+        nc.vector.tensor_copy(q_in[:], q_raw[:].rearrange("p t q -> p q t"))
+        q_codes = sb.tile([P, Q], U32, name="q_codes", align_bytes=64)
+        q_plane = sb.tile([P, Q], U8, name="q_plane", align_bytes=64)
+        nc.vector.quantize_mx(out=q_codes[:].bitcast(FP8X4), scales=q_plane[:], in_=q_in[:].rearrange("p q t -> p (q t)"))
+
+        pg = sb.tile([P, PLACES, Z], BF16, name="pg", tag="old_key2")
+        for t in range(PLACES - 1):
+            nc.vector.tensor_tensor(pg[:, t, :], kb_banks[t][:], f2[t][:], ALU.subtract)
+        halves = [slice(0, HALF), slice(HALF, Z)]
+        last = PLACES - 1
+        for cols in halves:
+            nc.vector.tensor_tensor(pg[:, last, cols], kb_banks[last][:, cols], f2[last][:, cols], ALU.subtract)
+        s = sb.tile([P, Z], F32, name="s")
+        pg_in = [sb.tile([P, HALF, PLACES], BF16, name="pg_in%d" % h, align_bytes=64) for h in range(2)]
+        nc.scalar.copy(pg_in[0][:].rearrange("p (c i) t -> p c t i", i=4), pg[:, :, halves[0]].rearrange("p t (c i) -> p c t i", i=4))
+        nc.vector.tensor_copy(pg_in[1][:].rearrange("p (c i) t -> p c t i", i=4), pg[:, :, halves[1]].rearrange("p t (c i) -> p c t i", i=4))
+        for h in (1, 0):
+            cols = halves[h]
+            pg_codes = sb.tile([P, HALF], U32, name="pg_codes%d" % h, align_bytes=64)
+            pg_plane = sb.tile([P, HALF], U8, name="pg_plane%d" % h, align_bytes=64)
+            nc.vector.quantize_mx(out=pg_codes[:].bitcast(FP8X4), scales=pg_plane[:], in_=pg_in[h][:].rearrange("p z t -> p (z t)"))
+            s_bank = ps.tile([P, 1, HALF], F32, name="s_bank%d" % h, tag=("bank_a", "bank_b")[h])
+            nc.tensor.matmul_mx(
+                out=s_bank[:, 0, :], lhsT=q_codes[:].bitcast(FP8X4), lhsT_scale=q_plane[:],
+                rhs=pg_codes[:].bitcast(FP8X4), rhs_scale=pg_plane[:], start=True, stop=True,
+            )
+            if h == 1:
+                nc.scalar.copy(s[:, cols], s_bank[:, 0, :])
+            else:
+                nc.vector.tensor_copy(s[:, cols], s_bank[:, 0, :])
+
+        plus = sb.tile([P, J], F32, name="plus")
+        minus = sb.tile([P, J], F32, name="minus")
+        res = sb.tile([P, J], F32, name="res")
+        nc.vector.tensor_copy(plus[:], s[:].indirect(plus_picks[:]))
+        nc.scalar.activation(minus[:], s[:].indirect(minus_picks[:]), COPY)
+        nc.vector.scalar_tensor_tensor(res[:], plus[:], 2.0, minus[:], ALU.mult, ALU.subtract)
+        nc.sync.dma_start(out, res[:])

@@ -37,48 +37,36 @@ def tile_attend_headcarry_plainq_kernel(
             nc.sync.dma_start(t[:], src)
             return t
 
-        def load_scale_rows(src, width, name, tag):
-            t = sb.tile([P, 2, width], U8, name=name, tag=tag, align_bytes=64)
-            nc.vector.memset(t[0:64].bitcast(I32), 0)
-            rows = src[0].bitcast(I32).rearrange("(h a f) c -> a f h c", h=2, a=2)
-            for a in range(2):
-                nc.sync.dma_start(t[32 * a : 32 * a + 4].bitcast(I32), rows[a])
+        def load_scale_stage(eng, src, width, name, parts, tag):
+            t = sb.tile([parts, 4, width // 4], I32, name=name, tag=tag, align_bytes=64)
+            eng.dma_start(t[0:4], src[0].bitcast(I32).rearrange("(a f) c -> f a c", f=4))
             return t
 
-        def load_scale_stage(src, width, name, tag):
-            t = sb.tile([4, 4, width // 4], I32, name=name, tag=tag, align_bytes=64)
-            nc.scalar.dma_start(t[:], src[0].bitcast(I32).rearrange("(a f) c -> f a c", f=4))
-            return t
-
-        def zeroed_plane(width, name):
-            t = sb.tile([P, width], U8, name=name, align_bytes=64)
-            nc.vector.memset(t[:].bitcast(I32), 0)
-            return t
-
-        def raise_upper(t):
-            nc.vector.tensor_copy(t[64:128, 0, :].bitcast(I32), t[0:64, 1, :].bitcast(I32))
-
-        def deal_scales(t, name):
-            plane = sb.tile([P, D], U8, name=name, align_bytes=64)
-            nc.vector.tensor_copy(
-                plane[:].bitcast(I32).rearrange("p (t g) -> p t g", t=PLACES),
-                t[:, 0, :].bitcast(I32).rearrange("p (g t) -> p t g", t=PLACES),
+        def spread_dealt(a, plane, rows):
+            eng = nc.gpsimd if a == 0 else nc.vector
+            eng.tensor_copy(
+                plane[32 * a : 32 * a + 4, :].rearrange("f (t g) -> f t g", t=PLACES),
+                rows[0:4, a, :].rearrange("f (g t) -> f t g", t=PLACES),
             )
-            return plane
 
-        wk_rows = load_scale_stage(wk_scales, D, "wk_rows", "slot0")
-        news_rows = load_scale_stage(news_scales, I, "news_rows", "news_rows")
-        wk_raw = sb.tile([P, D // 2], I32, name="wk_raw", tag="slot1", align_bytes=64)
+        def spread(a, plane, rows):
+            nc.vector.tensor_copy(plane[32 * a : 32 * a + 4, :], rows[0:4, a, :])
+
+        wk_rows = load_scale_stage(nc.scalar, wk_scales, D, "wk_rows", 4, "wk_rows")
+        news_rows = load_scale_stage(nc.scalar, news_scales, I, "news_rows", P, "slot3")
+        wp_rows = load_scale_stage(nc.scalar, wp_scales, D, "wp_rows", 4, "wp_rows")
+        wk_raw = sb.tile([P, D // 2], I32, name="wk_raw")
         nc.sync.dma_start(wk_raw[:], wk_words[0].bitcast(I32))
-        news_codes = sb.tile([P, I], I32, name="news_codes", tag="slot3", align_bytes=64)
+        news_codes = sb.tile([P, I], I32, name="news_codes", align_bytes=64)
         nc.sync.dma_start(news_codes[:], news_words[0].rearrange("p n t -> p (n t)").bitcast(I32))
         fresh_slots = load_list(offs, "fresh_slots")
-        wp_raw = sb.tile([P, D], I32, name="wp_raw", tag="fresh_key")
+        wp_raw = sb.tile([P, D], I32, name="wp_raw", tag="ring0", align_bytes=64)
         nc.sync.dma_start(wp_raw[:], wp_words[0].rearrange("p n t -> p (n t)").bitcast(I32))
-        olds_codes = sb.tile([P, Z // 2], I32, name="olds_codes", align_bytes=64)
+        olds_codes = sb.tile([P, Z // 2], I32, name="olds_codes", tag="slot2", align_bytes=64)
         nc.sync.dma_start(olds_codes[:], olds_words[0].bitcast(I32))
-        wp_rows = load_scale_rows(wp_scales, D, "wp_rows", "wp_rows")
-        olds_rows = load_scale_rows(olds_scales, Z, "olds_rows", "olds_rows")
+        olds_plane = sb.tile([P, Z // 4], I32, name="olds_plane", align_bytes=64)
+        for a in range(4):
+            nc.sync.dma_start(olds_plane[32 * a : 32 * a + 4, :], olds_scales[0].bitcast(I32)[4 * a : 4 * a + 4, :])
         old_picks = load_list(offs3, "old_picks")
         fresh_picks = load_list(offs2, "fresh_picks")
         q_raw = sb.tile([P, PLACES, Q], F32, name="q_raw")
@@ -88,24 +76,21 @@ def tile_attend_headcarry_plainq_kernel(
         plus_picks = load_list(offs4, "plus_picks")
         minus_picks = load_list(offs5, "minus_picks")
 
-        wk_plane = zeroed_plane(D, "wk_plane")
-        news_plane = zeroed_plane(I, "news_plane")
-        f1 = [sb.tile([P, Z], F32, name="f1_%d" % t) for t in range(PLACES)]
-        for t in range(PLACES):
+        wk_plane = sb.tile([P, D // 4], I32, name="wk_plane", align_bytes=64)
+        f1 = [sb.tile([P, Z], F32, name="f1_%d" % t) for t in range(PLACES - 1)]
+        for t in range(PLACES - 1):
             nc.vector.memset(f1[t][:], 0.0)
 
-        wk_codes = sb.tile([P, D], U16, name="wk_codes", tag="slot2", align_bytes=64)
-        nc.scalar.copy(
-            wk_codes[:].rearrange("p (t g r) -> p t g r", t=PLACES, r=RUN),
-            wk_raw[:].bitcast(U16).rearrange("p (g t r) -> p t g r", t=PLACES, r=RUN),
-        )
+        wk_first = sb.tile([P, P], U16, name="wk_first", tag="wk_first", align_bytes=64)
+        wk_rest = sb.tile([P, PLACES - 1, P], U16, name="wk_rest", align_bytes=64)
+        wk_dealt = wk_raw[:].bitcast(U16).rearrange("p (g t r) -> p t g r", t=PLACES, r=RUN)
+        nc.scalar.copy(wk_first[:].rearrange("p (g r) -> p g r", r=RUN), wk_dealt[:, 0])
+        nc.scalar.copy(wk_rest[:].rearrange("p t (g r) -> p t g r", r=RUN), wk_dealt[:, 1:PLACES])
+        wk_codes = [wk_first[:]] + [wk_rest[:, t, :] for t in range(PLACES - 1)]
         for a in range(4):
-            rows = slice(32 * a, 32 * a + 4)
-            nc.vector.tensor_copy(
-                wk_plane[rows, :].bitcast(I32).rearrange("f (t g) -> f t g", t=PLACES),
-                wk_rows[:, a, :].rearrange("f (g t) -> f t g", t=PLACES),
-            )
-            nc.vector.tensor_copy(news_plane[rows, :].bitcast(I32), news_rows[:, a, :])
+            spread_dealt(a, wk_plane, wk_rows)
+            if a > 0:
+                spread(a, news_rows[:, 0, :], news_rows)
 
         kn_banks = [
             ps.tile([P, 1, I], F32, name="kn_bank0", tag="bank_a"),
@@ -116,11 +101,21 @@ def tile_attend_headcarry_plainq_kernel(
         for t in range(PLACES):
             cols = slice(t * P, (t + 1) * P)
             nc.tensor.matmul_mx(
-                out=kn_slot[t], lhsT=wk_codes[:, cols].bitcast(FP4X4), lhsT_scale=wk_plane[:, cols],
-                rhs=news_codes[:].bitcast(FP8X4), rhs_scale=news_plane[:], start=True, stop=True,
+                out=kn_slot[t], lhsT=wk_codes[t].bitcast(FP4X4), lhsT_scale=wk_plane[:].bitcast(U8)[:, cols],
+                rhs=news_codes[:].bitcast(FP8X4), rhs_scale=news_rows[:, 0, :].bitcast(U8), start=True, stop=True,
             )
-        kn0 = sb.tile([P, 1, I], F32, name="kn0")
-        kn1 = sb.tile([P, 1, I], F32, name="kn1")
+        wp_plane = sb.tile([P, D // 4], I32, name="wp_plane", tag="wk_first", align_bytes=64)
+        for a in (0, 3, 2, 1):
+            spread_dealt(a, wp_plane, wp_rows)
+        f1.append(sb.tile([P, Z], F32, name="f1_3", tag="wp_rows", align_bytes=64))
+        nc.gpsimd.memset(f1[3][:], 0.0)
+        wp_codes = sb.tile([P, D], I32, name="wp_codes", tag="slot3", align_bytes=64)
+        nc.vector.tensor_copy(
+            wp_codes[:].rearrange("p (t g r) -> p t g r", t=PLACES, r=RUN),
+            wp_raw[:].rearrange("p (g t r) -> p t g r", t=PLACES, r=RUN),
+        )
+        kn0 = sb.tile([P, 1, I], F32, name="kn0", tag="slot0", align_bytes=64)
+        kn1 = sb.tile([P, 1, I], F32, name="kn1", tag="slot1", align_bytes=64)
         kn23 = sb.tile([P, 2, I], F32, name="kn23")
         nc.scalar.copy(kn0[:], kn_banks[0][:])
         nc.vector.tensor_copy(kn1[:], kn_banks[1][:])
@@ -129,32 +124,25 @@ def tile_attend_headcarry_plainq_kernel(
         for t in range(PLACES):
             nc.scalar.activation(f1[t][:].indirect(fresh_slots[:]), kn[t], COPY)
 
-        f2 = [sb.tile([P, Z], F32, name="f2_%d" % t, tag="slot%d" % t, align_bytes=64) for t in range(PLACES)]
-        for t in range(PLACES):
-            nc.vector.memset(f2[t][:], 0.0)
-
-        raise_upper(wp_rows)
-        raise_upper(olds_rows)
-        wp_codes = sb.tile([P, D], I32, name="wp_codes", align_bytes=64)
-        nc.vector.tensor_copy(
-            wp_codes[:].rearrange("p (t g r) -> p t g r", t=PLACES, r=RUN),
-            wp_raw[:].rearrange("p (g t r) -> p t g r", t=PLACES, r=RUN),
-        )
-        wp_plane = deal_scales(wp_rows, "wp_plane")
         kb_banks = [ps.tile([P, Z], F32, name="kb_bank%d" % t) for t in range(PLACES)]
         for t in range(PLACES):
             cols = slice(t * P, (t + 1) * P)
             nc.tensor.matmul_mx(
-                out=kb_banks[t][:], lhsT=wp_codes[:, cols].bitcast(FP8X4), lhsT_scale=wp_plane[:, cols],
-                rhs=olds_codes[:].bitcast(U16).bitcast(FP4X4), rhs_scale=olds_rows[:, 0, :], start=True, stop=True,
+                out=kb_banks[t][:], lhsT=wp_codes[:, cols].bitcast(FP8X4), lhsT_scale=wp_plane[:].bitcast(U8)[:, cols],
+                rhs=olds_codes[:].bitcast(U16).bitcast(FP4X4), rhs_scale=olds_plane[:].bitcast(U8), start=True, stop=True,
             )
-        kb = [sb.tile([P, Z], F32, name="kb%d" % t) for t in range(PLACES)]
+        f2 = [sb.tile([P, Z], F32, name="f2_%d" % t, tag="slot%d" % t, align_bytes=64) for t in range(PLACES)]
+        for t in range(PLACES):
+            nc.gpsimd.memset(f2[t][:], 0.0)
+
+        kb = [sb.tile([P, Z], F32, name="kb0", tag="ring1", align_bytes=64)]
+        kb.extend([sb.tile([P, Z], F32, name="kb%d" % t) for t in range(1, PLACES)])
         old_key = [sb.tile([P, J], F32, name="old_key%d" % t, tag="old_key%d" % t) for t in range(PLACES)]
         w = [sb.tile([P, J], F32, name="w%d" % t) for t in range(PLACES)]
         nc.vector.tensor_copy(kb[0][:], kb_banks[0][:])
         for t in range(PLACES):
             nc.vector.tensor_copy(old_key[t][:], kb[t][:].indirect(old_picks[:]))
-            fresh_key = sb.tile([P, J], F32, name="fresh_key", tag="fresh_key")
+            fresh_key = sb.tile([P, J], F32, name="fresh_key", tag="ring%d" % (t % 2), align_bytes=64)
             nc.vector.tensor_copy(fresh_key[:], f1[t][:].indirect(fresh_picks[:]))
             if t + 1 < PLACES:
                 nc.vector.tensor_copy(kb[t + 1][:], kb_banks[t + 1][:])
@@ -162,22 +150,25 @@ def tile_attend_headcarry_plainq_kernel(
             nc.scalar.activation(f2[t][:].indirect(old_picks[:]), w[t][:], COPY)
 
         q_in = sb.tile([P, Q, PLACES], BF16, name="q_in", align_bytes=64)
-        nc.vector.tensor_copy(q_in[:], q_raw[:].rearrange("p t q -> p q t"))
-        q_codes = sb.tile([P, Q], U32, name="q_codes", align_bytes=64)
+        nc.gpsimd.tensor_scalar(q_in[:], q_raw[:].rearrange("p t q -> p q t"), 1.0, 0.0, ALU.mult, ALU.add)
+        q_codes = sb.tile([P, Q], U32, name="q_codes", tag="ring1", align_bytes=64)
         q_plane = sb.tile([P, Q], U8, name="q_plane", align_bytes=64)
         nc.vector.quantize_mx(out=q_codes[:].bitcast(FP8X4), scales=q_plane[:], in_=q_in[:].rearrange("p q t -> p (q t)"))
 
-        pg = sb.tile([P, PLACES, Z], BF16, name="pg", tag="old_key2")
-        for t in range(PLACES - 1):
-            nc.vector.tensor_tensor(pg[:, t, :], kb_banks[t][:], f2[t][:], ALU.subtract)
+        pg = sb.tile([P, PLACES, Z], BF16, name="pg", tag="old_key3")
         halves = [slice(0, HALF), slice(HALF, Z)]
+        pg_in = [sb.tile([P, HALF, PLACES], BF16, name="pg_in%d" % h, align_bytes=64) for h in range(2)]
+        for t in range(2):
+            nc.vector.tensor_tensor(pg[:, t, :], kb_banks[t][:], f2[t][:], ALU.subtract)
+        for h in range(2):
+            nc.vector.tensor_copy(pg_in[h][:, :, 0:2], pg[:, 0:2, halves[h]].rearrange("p t z -> p z t"))
+        nc.vector.tensor_tensor(pg[:, 2, :], kb_banks[2][:], f2[2][:], ALU.subtract)
         last = PLACES - 1
         for cols in halves:
             nc.vector.tensor_tensor(pg[:, last, cols], kb_banks[last][:, cols], f2[last][:, cols], ALU.subtract)
         s = sb.tile([P, Z], F32, name="s")
-        pg_in = [sb.tile([P, HALF, PLACES], BF16, name="pg_in%d" % h, align_bytes=64) for h in range(2)]
-        nc.scalar.copy(pg_in[0][:].rearrange("p (c i) t -> p c t i", i=4), pg[:, :, halves[0]].rearrange("p t (c i) -> p c t i", i=4))
-        nc.vector.tensor_copy(pg_in[1][:].rearrange("p (c i) t -> p c t i", i=4), pg[:, :, halves[1]].rearrange("p t (c i) -> p c t i", i=4))
+        nc.scalar.copy(pg_in[0][:, :, 2:4], pg[:, 2:4, halves[0]].rearrange("p t z -> p z t"))
+        nc.vector.tensor_copy(pg_in[1][:, :, 2:4], pg[:, 2:4, halves[1]].rearrange("p t z -> p z t"))
         for h in (1, 0):
             cols = halves[h]
             pg_codes = sb.tile([P, HALF], U32, name="pg_codes%d" % h, align_bytes=64)
@@ -193,10 +184,12 @@ def tile_attend_headcarry_plainq_kernel(
             else:
                 nc.vector.tensor_copy(s[:, cols], s_bank[:, 0, :])
 
-        plus = sb.tile([P, J], F32, name="plus")
-        minus = sb.tile([P, J], F32, name="minus")
-        res = sb.tile([P, J], F32, name="res")
-        nc.vector.tensor_copy(plus[:], s[:].indirect(plus_picks[:]))
-        nc.scalar.activation(minus[:], s[:].indirect(minus_picks[:]), COPY)
-        nc.vector.scalar_tensor_tensor(res[:], plus[:], 2.0, minus[:], ALU.mult, ALU.subtract)
-        nc.sync.dma_start(out, res[:])
+        plus = [sb.tile([P, J // 2], F32, name="plus%d" % h) for h in range(2)]
+        minus = [sb.tile([P, J // 2], F32, name="minus%d" % h) for h in range(2)]
+        res = [sb.tile([P, J // 2], F32, name="res%d" % h) for h in range(2)]
+        for h in range(2):
+            nc.vector.tensor_copy(plus[h][:], s[:].indirect(plus_picks[:, 8 * h : 8 * h + 8]))
+            nc.scalar.activation(minus[h][:], s[:].indirect(minus_picks[:, 8 * h : 8 * h + 8]), COPY)
+        for h in range(2):
+            nc.vector.scalar_tensor_tensor(res[h][:], plus[h][:], 2.0, minus[h][:], ALU.mult, ALU.subtract)
+            nc.sync.dma_start(out[:, h * (J // 2) : (h + 1) * (J // 2)], res[h][:])

@@ -17,7 +17,7 @@ C, D, I, Z, J, Q = 512, 512, 256, 512, 256, 128
 P = 128
 PLACES = 4
 RUN = 4
-HALF = Z // 2
+PIECE = 128
 
 FLOPS = 2 * C * D * Z + 2 * C * D * I + 2 * D * Q * Z
 
@@ -43,8 +43,7 @@ def tile_attend_headcarry_plainq_kernel(
             return t
 
         def spread_dealt(a, plane, rows):
-            eng = nc.gpsimd if a == 0 else nc.vector
-            eng.tensor_copy(
+            nc.vector.tensor_copy(
                 plane[32 * a : 32 * a + 4, :].rearrange("f (t g) -> f t g", t=PLACES),
                 rows[0:4, a, :].rearrange("f (g t) -> f t g", t=PLACES),
             )
@@ -62,7 +61,7 @@ def tile_attend_headcarry_plainq_kernel(
         fresh_slots = load_list(offs, "fresh_slots")
         wp_raw = sb.tile([P, D], I32, name="wp_raw", tag="ring0", align_bytes=64)
         nc.sync.dma_start(wp_raw[:], wp_words[0].rearrange("p n t -> p (n t)").bitcast(I32))
-        olds_codes = sb.tile([P, Z // 2], I32, name="olds_codes", tag="slot2", align_bytes=64)
+        olds_codes = sb.tile([P, Z // 2], I32, name="olds_codes", align_bytes=64)
         nc.sync.dma_start(olds_codes[:], olds_words[0].bitcast(I32))
         olds_plane = sb.tile([P, Z // 4], I32, name="olds_plane", align_bytes=64)
         for a in range(4):
@@ -77,9 +76,10 @@ def tile_attend_headcarry_plainq_kernel(
         minus_picks = load_list(offs5, "minus_picks")
 
         wk_plane = sb.tile([P, D // 4], I32, name="wk_plane", align_bytes=64)
-        f1 = [sb.tile([P, Z], F32, name="f1_%d" % t) for t in range(PLACES - 1)]
-        for t in range(PLACES - 1):
-            nc.vector.memset(f1[t][:], 0.0)
+        f1 = [sb.tile([P, Z], F32, name="f1_%d" % t) for t in range(PLACES)]
+        f2 = [sb.tile([P, Z], F32, name="f2_%d" % t) for t in range(PLACES - 1)]
+        for window in f1 + f2:
+            nc.vector.memset(window[:].bitcast(I32), 0)
 
         wk_first = sb.tile([P, P], U16, name="wk_first", tag="wk_first", align_bytes=64)
         wk_rest = sb.tile([P, PLACES - 1, P], U16, name="wk_rest", align_bytes=64)
@@ -91,6 +91,9 @@ def tile_attend_headcarry_plainq_kernel(
             spread_dealt(a, wk_plane, wk_rows)
             if a > 0:
                 spread(a, news_rows[:, 0, :], news_rows)
+
+        f2.append(sb.tile([P, Z], F32, name="f2_3", tag="wk_rows", align_bytes=64))
+        nc.vector.memset(f2[3][:].bitcast(I32), 0)
 
         kn_banks = [
             ps.tile([P, 1, I], F32, name="kn_bank0", tag="bank_a"),
@@ -107,15 +110,13 @@ def tile_attend_headcarry_plainq_kernel(
         wp_plane = sb.tile([P, D // 4], I32, name="wp_plane", tag="wk_first", align_bytes=64)
         for a in (0, 3, 2, 1):
             spread_dealt(a, wp_plane, wp_rows)
-        f1.append(sb.tile([P, Z], F32, name="f1_3", tag="wp_rows", align_bytes=64))
-        nc.gpsimd.memset(f1[3][:], 0.0)
         wp_codes = sb.tile([P, D], I32, name="wp_codes", tag="slot3", align_bytes=64)
         nc.vector.tensor_copy(
             wp_codes[:].rearrange("p (t g r) -> p t g r", t=PLACES, r=RUN),
             wp_raw[:].rearrange("p (g t r) -> p t g r", t=PLACES, r=RUN),
         )
-        kn0 = sb.tile([P, 1, I], F32, name="kn0", tag="slot0", align_bytes=64)
-        kn1 = sb.tile([P, 1, I], F32, name="kn1", tag="slot1", align_bytes=64)
+        kn0 = sb.tile([P, 1, I], F32, name="kn0")
+        kn1 = sb.tile([P, 1, I], F32, name="kn1")
         kn23 = sb.tile([P, 2, I], F32, name="kn23")
         nc.scalar.copy(kn0[:], kn_banks[0][:])
         nc.vector.tensor_copy(kn1[:], kn_banks[1][:])
@@ -131,10 +132,6 @@ def tile_attend_headcarry_plainq_kernel(
                 out=kb_banks[t][:], lhsT=wp_codes[:, cols].bitcast(FP8X4), lhsT_scale=wp_plane[:].bitcast(U8)[:, cols],
                 rhs=olds_codes[:].bitcast(U16).bitcast(FP4X4), rhs_scale=olds_plane[:].bitcast(U8), start=True, stop=True,
             )
-        f2 = [sb.tile([P, Z], F32, name="f2_%d" % t, tag="slot%d" % t, align_bytes=64) for t in range(PLACES)]
-        for t in range(PLACES):
-            nc.gpsimd.memset(f2[t][:], 0.0)
-
         kb = [sb.tile([P, Z], F32, name="kb0", tag="ring1", align_bytes=64)]
         kb.extend([sb.tile([P, Z], F32, name="kb%d" % t) for t in range(1, PLACES)])
         old_key = [sb.tile([P, J], F32, name="old_key%d" % t, tag="old_key%d" % t) for t in range(PLACES)]
@@ -149,40 +146,41 @@ def tile_attend_headcarry_plainq_kernel(
             nc.vector.tensor_tensor(w[t][:], fresh_key[:], old_key[t][:], ALU.max)
             nc.scalar.activation(f2[t][:].indirect(old_picks[:]), w[t][:], COPY)
 
-        q_in = sb.tile([P, Q, PLACES], BF16, name="q_in", align_bytes=64)
-        nc.gpsimd.tensor_scalar(q_in[:], q_raw[:].rearrange("p t q -> p q t"), 1.0, 0.0, ALU.mult, ALU.add)
+        q_in = sb.tile([P, Q, PLACES], BF16, name="q_in", tag="ring0", align_bytes=64)
+        nc.vector.tensor_copy(q_in[:].rearrange("p (c i) t -> p c t i", i=4), q_raw[:].rearrange("p t (c i) -> p c t i", i=4))
         q_codes = sb.tile([P, Q], U32, name="q_codes", tag="ring1", align_bytes=64)
         q_plane = sb.tile([P, Q], U8, name="q_plane", align_bytes=64)
         nc.vector.quantize_mx(out=q_codes[:].bitcast(FP8X4), scales=q_plane[:], in_=q_in[:].rearrange("p q t -> p (q t)"))
 
         pg = sb.tile([P, PLACES, Z], BF16, name="pg", tag="old_key3")
-        halves = [slice(0, HALF), slice(HALF, Z)]
-        pg_in = [sb.tile([P, HALF, PLACES], BF16, name="pg_in%d" % h, align_bytes=64) for h in range(2)]
-        for t in range(2):
+        pieces = [slice(n * PIECE, (n + 1) * PIECE) for n in range(Z // PIECE)]
+        for t in range(PLACES - 1):
             nc.vector.tensor_tensor(pg[:, t, :], kb_banks[t][:], f2[t][:], ALU.subtract)
-        for h in range(2):
-            nc.vector.tensor_copy(pg_in[h][:, :, 0:2], pg[:, 0:2, halves[h]].rearrange("p t z -> p z t"))
-        nc.vector.tensor_tensor(pg[:, 2, :], kb_banks[2][:], f2[2][:], ALU.subtract)
         last = PLACES - 1
-        for cols in halves:
+        for cols in pieces:
             nc.vector.tensor_tensor(pg[:, last, cols], kb_banks[last][:, cols], f2[last][:, cols], ALU.subtract)
+        pg_in = [sb.tile([P, PIECE, PLACES], BF16, name="pg_in%d" % n, align_bytes=64) for n in range(4)]
+        for n in range(4):
+            dst = pg_in[n][:].rearrange("p (c i) t -> p c t i", i=4)
+            src = pg[:, :, pieces[n]].rearrange("p t (c i) -> p c t i", i=4)
+            if n < 2:
+                nc.scalar.copy(dst, src)
+            else:
+                nc.vector.tensor_copy(dst, src)
         s = sb.tile([P, Z], F32, name="s")
-        nc.scalar.copy(pg_in[0][:, :, 2:4], pg[:, 2:4, halves[0]].rearrange("p t z -> p z t"))
-        nc.vector.tensor_copy(pg_in[1][:, :, 2:4], pg[:, 2:4, halves[1]].rearrange("p t z -> p z t"))
-        for h in (1, 0):
-            cols = halves[h]
-            pg_codes = sb.tile([P, HALF], U32, name="pg_codes%d" % h, align_bytes=64)
-            pg_plane = sb.tile([P, HALF], U8, name="pg_plane%d" % h, align_bytes=64)
-            nc.vector.quantize_mx(out=pg_codes[:].bitcast(FP8X4), scales=pg_plane[:], in_=pg_in[h][:].rearrange("p z t -> p (z t)"))
-            s_bank = ps.tile([P, 1, HALF], F32, name="s_bank%d" % h, tag=("bank_a", "bank_b")[h])
+        for n in (0, 2, 3, 1):
+            pg_codes = sb.tile([P, PIECE], U32, name="pg_codes%d" % n, align_bytes=64)
+            pg_plane = sb.tile([P, PIECE], U8, name="pg_plane%d" % n, align_bytes=64)
+            nc.vector.quantize_mx(out=pg_codes[:].bitcast(FP8X4), scales=pg_plane[:], in_=pg_in[n][:].rearrange("p z t -> p (z t)"))
+            s_bank = ps.tile([P, 1, PIECE], F32, name="s_bank%d" % n, tag=("bank_a", "bank_b", "bank_c", "bank_d")[n])
             nc.tensor.matmul_mx(
                 out=s_bank[:, 0, :], lhsT=q_codes[:].bitcast(FP8X4), lhsT_scale=q_plane[:],
                 rhs=pg_codes[:].bitcast(FP8X4), rhs_scale=pg_plane[:], start=True, stop=True,
             )
-            if h == 1:
-                nc.scalar.copy(s[:, cols], s_bank[:, 0, :])
+            if n != 1:
+                nc.scalar.copy(s[:, pieces[n]], s_bank[:, 0, :])
             else:
-                nc.vector.tensor_copy(s[:, cols], s_bank[:, 0, :])
+                nc.vector.tensor_copy(s[:, pieces[n]], s_bank[:, 0, :])
 
         plus = [sb.tile([P, J // 2], F32, name="plus%d" % h) for h in range(2)]
         minus = [sb.tile([P, J // 2], F32, name="minus%d" % h) for h in range(2)]

from contextlib import ExitStack

import concourse.mybir as mybir

F32 = mybir.dt.float32
BF16 = mybir.dt.bfloat16
I32 = mybir.dt.int32
U32 = mybir.dt.uint32
U16 = mybir.dt.uint16
U8 = mybir.dt.uint8
FP8X4 = mybir.dt.float8_e4m3fn_x4
FP4X4 = mybir.dt.float4_e2m1fn_x4
ALU = mybir.AluOpType
COPY = mybir.ActivationFunctionType.Copy

C, D, I, Z, J, Q = 512, 512, 256, 512, 256, 128
P = 128
PLACES = 4
RUN = 4
PIECE = 128

FLOPS = 2 * C * D * Z + 2 * C * D * I + 2 * D * Q * Z


def tile_attend_headcarry_plainq_kernel(
    tc, wp_words, wp_scales, olds_words, olds_scales, wk_words, wk_scales, news_words, news_scales,
    query, offs, offs2, offs3, offs4, offs5, out,
):
    nc = tc.nc
    with ExitStack() as ctx:
        lists = ctx.enter_context(tc.tile_pool(name="lists", bufs=1))
        sb = ctx.enter_context(tc.tile_pool(name="sb", bufs=1))
        ps = ctx.enter_context(tc.psum_pool(name="ps", bufs=1))

        def load_list(src, name):
            t = lists.tile([P, 16], U16, name=name)
            nc.sync.dma_start(t[:], src)
            return t

        def load_scale_stage(eng, src, width, name, parts, tag):
            t = sb.tile([parts, 4, width // 4], I32, name=name, tag=tag, align_bytes=64)
            eng.dma_start(t[0:4], src[0].bitcast(I32).rearrange("(a f) c -> f a c", f=4))
            return t

        def spread_dealt(a, plane, rows):
            nc.vector.tensor_copy(
                plane[32 * a : 32 * a + 4, :].rearrange("f (t g) -> f t g", t=PLACES),
                rows[0:4, a, :].rearrange("f (g t) -> f t g", t=PLACES),
            )

        def spread(a, plane, rows):
            nc.vector.tensor_copy(plane[32 * a : 32 * a + 4, :], rows[0:4, a, :])

        wk_rows = load_scale_stage(nc.scalar, wk_scales, D, "wk_rows", 4, "wk_rows")
        news_rows = load_scale_stage(nc.scalar, news_scales, I, "news_rows", P, "slot3")
        wp_rows = load_scale_stage(nc.scalar, wp_scales, D, "wp_rows", 4, "wp_rows")
        wk_raw = sb.tile([P, D // 2], I32, name="wk_raw")
        nc.sync.dma_start(wk_raw[:], wk_words[0].bitcast(I32))
        news_codes = sb.tile([P, I], I32, name="news_codes", align_bytes=64)
        nc.sync.dma_start(news_codes[:], news_words[0].rearrange("p n t -> p (n t)").bitcast(I32))
        fresh_slots = load_list(offs, "fresh_slots")
        wp_raw = sb.tile([P, D], I32, name="wp_raw", tag="ring0", align_bytes=64)
        nc.sync.dma_start(wp_raw[:], wp_words[0].rearrange("p n t -> p (n t)").bitcast(I32))
        olds_codes = sb.tile([P, Z // 2], I32, name="olds_codes", align_bytes=64)
        nc.sync.dma_start(olds_codes[:], olds_words[0].bitcast(I32))
        olds_plane = sb.tile([P, Z // 4], I32, name="olds_plane", align_bytes=64)
        for a in range(4):
            nc.sync.dma_start(olds_plane[32 * a : 32 * a + 4, :], olds_scales[0].bitcast(I32)[4 * a : 4 * a + 4, :])
        old_picks = load_list(offs3, "old_picks")
        fresh_picks = load_list(offs2, "fresh_picks")
        q_raw = sb.tile([P, PLACES, Q], F32, name="q_raw")
        q_rows = query.rearrange("(g t r) q -> r g t q", t=PLACES, r=RUN)
        for r in range(RUN):
            nc.sync.dma_start(q_raw[r:P:RUN, :, :], q_rows[r])
        plus_picks = load_list(offs4, "plus_picks")
        minus_picks = load_list(offs5, "minus_picks")

        wk_plane = sb.tile([P, D // 4], I32, name="wk_plane", align_bytes=64)
        f1 = [sb.tile([P, Z], F32, name="f1_%d" % t) for t in range(PLACES)]
        f2 = [sb.tile([P, Z], F32, name="f2_%d" % t) for t in range(PLACES - 1)]
        for window in f1 + f2:
            nc.vector.memset(window[:].bitcast(I32), 0)

        wk_first = sb.tile([P, P], U16, name="wk_first", tag="wk_first", align_bytes=64)
        wk_rest = sb.tile([P, PLACES - 1, P], U16, name="wk_rest", align_bytes=64)
        wk_dealt = wk_raw[:].bitcast(U16).rearrange("p (g t r) -> p t g r", t=PLACES, r=RUN)
        nc.scalar.copy(wk_first[:].rearrange("p (g r) -> p g r", r=RUN), wk_dealt[:, 0])
        nc.scalar.copy(wk_rest[:].rearrange("p t (g r) -> p t g r", r=RUN), wk_dealt[:, 1:PLACES])
        wk_codes = [wk_first[:]] + [wk_rest[:, t, :] for t in range(PLACES - 1)]
        for a in range(4):
            spread_dealt(a, wk_plane, wk_rows)
            if a > 0:
                spread(a, news_rows[:, 0, :], news_rows)

        f2.append(sb.tile([P, Z], F32, name="f2_3", tag="wk_rows", align_bytes=64))
        nc.vector.memset(f2[3][:].bitcast(I32), 0)

        kn_banks = [
            ps.tile([P, 1, I], F32, name="kn_bank0", tag="bank_a"),
            ps.tile([P, 1, I], F32, name="kn_bank1", tag="bank_b"),
            ps.tile([P, 2, I], F32, name="kn_bank2", tag="bank_c"),
        ]
        kn_slot = [kn_banks[0][:, 0, :], kn_banks[1][:, 0, :], kn_banks[2][:, 0, :], kn_banks[2][:, 1, :]]
        for t in range(PLACES):
            cols = slice(t * P, (t + 1) * P)
            nc.tensor.matmul_mx(
                out=kn_slot[t], lhsT=wk_codes[t].bitcast(FP4X4), lhsT_scale=wk_plane[:].bitcast(U8)[:, cols],
                rhs=news_codes[:].bitcast(FP8X4), rhs_scale=news_rows[:, 0, :].bitcast(U8), start=True, stop=True,
            )
        wp_plane = sb.tile([P, D // 4], I32, name="wp_plane", tag="wk_first", align_bytes=64)
        for a in (0, 3, 2, 1):
            spread_dealt(a, wp_plane, wp_rows)
        wp_codes = sb.tile([P, D], I32, name="wp_codes", tag="slot3", align_bytes=64)
        nc.vector.tensor_copy(
            wp_codes[:].rearrange("p (t g r) -> p t g r", t=PLACES, r=RUN),
            wp_raw[:].rearrange("p (g t r) -> p t g r", t=PLACES, r=RUN),
        )
        kn0 = sb.tile([P, 1, I], F32, name="kn0")
        kn1 = sb.tile([P, 1, I], F32, name="kn1")
        kn23 = sb.tile([P, 2, I], F32, name="kn23")
        nc.scalar.copy(kn0[:], kn_banks[0][:])
        nc.vector.tensor_copy(kn1[:], kn_banks[1][:])
        nc.vector.tensor_copy(kn23[:], kn_banks[2][:])
        kn = [kn0[:, 0, :], kn1[:, 0, :], kn23[:, 0, :], kn23[:, 1, :]]
        for t in range(PLACES):
            nc.scalar.activation(f1[t][:].indirect(fresh_slots[:]), kn[t], COPY)

        kb_banks = [ps.tile([P, Z], F32, name="kb_bank%d" % t) for t in range(PLACES)]
        for t in range(PLACES):
            cols = slice(t * P, (t + 1) * P)
            nc.tensor.matmul_mx(
                out=kb_banks[t][:], lhsT=wp_codes[:, cols].bitcast(FP8X4), lhsT_scale=wp_plane[:].bitcast(U8)[:, cols],
                rhs=olds_codes[:].bitcast(U16).bitcast(FP4X4), rhs_scale=olds_plane[:].bitcast(U8), start=True, stop=True,
            )
        kb = [sb.tile([P, Z], F32, name="kb0", tag="ring1", align_bytes=64)]
        kb.extend([sb.tile([P, Z], F32, name="kb%d" % t) for t in range(1, PLACES)])
        old_key = [sb.tile([P, J], F32, name="old_key%d" % t, tag="old_key%d" % t) for t in range(PLACES)]
        w = [sb.tile([P, J], F32, name="w%d" % t) for t in range(PLACES)]
        nc.vector.tensor_copy(kb[0][:], kb_banks[0][:])
        for t in range(PLACES):
            nc.vector.tensor_copy(old_key[t][:], kb[t][:].indirect(old_picks[:]))
            fresh_key = sb.tile([P, J], F32, name="fresh_key", tag="ring%d" % (t % 2), align_bytes=64)
            nc.vector.tensor_copy(fresh_key[:], f1[t][:].indirect(fresh_picks[:]))
            if t + 1 < PLACES:
                nc.vector.tensor_copy(kb[t + 1][:], kb_banks[t + 1][:])
            nc.vector.tensor_tensor(w[t][:], fresh_key[:], old_key[t][:], ALU.max)
            nc.scalar.activation(f2[t][:].indirect(old_picks[:]), w[t][:], COPY)

        q_in = sb.tile([P, Q, PLACES], BF16, name="q_in", tag="ring0", align_bytes=64)
        nc.vector.tensor_copy(q_in[:].rearrange("p (c i) t -> p c t i", i=4), q_raw[:].rearrange("p t (c i) -> p c t i", i=4))
        q_codes = sb.tile([P, Q], U32, name="q_codes", tag="ring1", align_bytes=64)
        q_plane = sb.tile([P, Q], U8, name="q_plane", align_bytes=64)
        nc.vector.quantize_mx(out=q_codes[:].bitcast(FP8X4), scales=q_plane[:], in_=q_in[:].rearrange("p q t -> p (q t)"))

        pg = sb.tile([P, PLACES, Z], BF16, name="pg", tag="old_key3")
        pieces = [slice(n * PIECE, (n + 1) * PIECE) for n in range(Z // PIECE)]
        for t in range(PLACES - 1):
            nc.vector.tensor_tensor(pg[:, t, :], kb_banks[t][:], f2[t][:], ALU.subtract)
        last = PLACES - 1
        for cols in pieces:
            nc.vector.tensor_tensor(pg[:, last, cols], kb_banks[last][:, cols], f2[last][:, cols], ALU.subtract)
        pg_in = [sb.tile([P, PIECE, PLACES], BF16, name="pg_in%d" % n, align_bytes=64) for n in range(4)]
        for n in range(4):
            dst = pg_in[n][:].rearrange("p (c i) t -> p c t i", i=4)
            src = pg[:, :, pieces[n]].rearrange("p t (c i) -> p c t i", i=4)
            if n < 2:
                nc.scalar.copy(dst, src)
            else:
                nc.vector.tensor_copy(dst, src)
        s = sb.tile([P, Z], F32, name="s")
        for n in (0, 2, 3, 1):
            pg_codes = sb.tile([P, PIECE], U32, name="pg_codes%d" % n, align_bytes=64)
            pg_plane = sb.tile([P, PIECE], U8, name="pg_plane%d" % n, align_bytes=64)
            nc.vector.quantize_mx(out=pg_codes[:].bitcast(FP8X4), scales=pg_plane[:], in_=pg_in[n][:].rearrange("p z t -> p (z t)"))
            s_bank = ps.tile([P, 1, PIECE], F32, name="s_bank%d" % n, tag=("bank_a", "bank_b", "bank_c", "bank_d")[n])
            nc.tensor.matmul_mx(
                out=s_bank[:, 0, :], lhsT=q_codes[:].bitcast(FP8X4), lhsT_scale=q_plane[:],
                rhs=pg_codes[:].bitcast(FP8X4), rhs_scale=pg_plane[:], start=True, stop=True,
            )
            if n != 1:
                nc.scalar.copy(s[:, pieces[n]], s_bank[:, 0, :])
            else:
                nc.vector.tensor_copy(s[:, pieces[n]], s_bank[:, 0, :])

        plus = [sb.tile([P, J // 2], F32, name="plus%d" % h) for h in range(2)]
        minus = [sb.tile([P, J // 2], F32, name="minus%d" % h) for h in range(2)]
        res = [sb.tile([P, J // 2], F32, name="res%d" % h) for h in range(2)]
        for h in range(2):
            nc.vector.tensor_copy(plus[h][:], s[:].indirect(plus_picks[:, 8 * h : 8 * h + 8]))
            nc.scalar.activation(minus[h][:], s[:].indirect(minus_picks[:, 8 * h : 8 * h + 8]), COPY)
        for h in range(2):
            nc.vector.scalar_tensor_tensor(res[h][:], plus[h][:], 2.0, minus[h][:], ALU.mult, ALU.subtract)
            nc.sync.dma_start(out[:, h * (J // 2) : (h + 1) * (J // 2)], res[h][:])
